import numpy as np
import ml_dtypes


def mxq(x, axis, fmt="e4m3"):
    dtype, down = {"e4m3": (ml_dtypes.float8_e4m3fn, 7), "e5m2": (ml_dtypes.float8_e5m2, 14)}[fmt]
    v = np.moveaxis(np.asarray(x, np.float32).astype(ml_dtypes.bfloat16).astype(np.float64), axis, -1)
    blocks = v.reshape(v.shape[:-1] + (-1, 32))
    amax = np.abs(blocks).max(-1, keepdims=True)
    byte = np.maximum(np.where(amax > 0, np.frexp(amax)[1] - 1 + 127, 0) - down, 1)
    scale = np.exp2(byte - 127.0)
    codes = (blocks / scale).astype(np.float32).astype(dtype).astype(np.float64)
    return np.moveaxis((codes * scale).reshape(v.shape), -1, axis)


WIDE = False


def mx_kscale(k):
    if not WIDE:
        return np.ones(k)
    levels = np.array([10, -10, 5, -5, 0])
    if k % 512:
        return np.exp2(np.random.permutation(np.resize(levels, k // 32))).repeat(32)
    a = np.empty((k // 512, 16))
    for p in range(k // 512):
        a[p, :8] = np.random.permutation(np.resize(levels, 8))
        for g in range(8):
            far = levels[np.abs(levels - a[p, g]) >= 10]
            a[p, g + 8] = far[np.random.randint(len(far))]
    return np.exp2(a.ravel()).repeat(32)


def f64(x):
    return np.asarray(x).astype(np.float64)


def striped(idx):
    return np.tile(np.asarray(idx).reshape(-1, 16).T, (8, 1)).astype(np.uint16)


def unstriped(offs):
    return offs[:16].T.reshape(-1).astype(np.int64)


def striped8(idx):
    return np.asarray(idx).reshape(8, -1, 16).transpose(0, 2, 1).reshape(128, -1).astype(np.uint16)


def unstriped8(offs):
    return offs.reshape(8, 16, -1).transpose(0, 2, 1).reshape(8, -1).astype(np.int64)


def pick8(x, idx, run):
    r = np.arange(len(x))
    return x[r[:, None], idx[r % (8 * run) // run]]


E2M1 = np.array([0.0, 0.5, 1.0, 1.5, 2.0, 3.0, 4.0, 6.0, -0.0, -0.5, -1.0, -1.5, -2.0, -3.0, -4.0, -6.0])


def pack_weight(w, fmt):
    k, n = w.shape
    w = f64(np.asarray(w, np.float32).astype(ml_dtypes.bfloat16)).reshape(k // 32, 32, n)
    amax = np.abs(w).max(1)
    if fmt == "e4m3":
        byte = np.frexp(amax)[1] - 1 + 127 - 7
    else:
        mant, ex = np.frexp(amax / 6.0)
        byte = np.where(mant > 0.5, ex, ex - 1) + 127
    byte = np.clip(np.where(amax > 0, byte, 1), 1, 254)
    scaled = (w * np.exp2(127.0 - byte)[:, None, :]).reshape(k, n).astype(np.float32)
    by_word = np.ascontiguousarray(scaled.reshape(k // 512, 128, 4, n).transpose(0, 1, 3, 2))
    if fmt == "e4m3":
        words = by_word.astype(ml_dtypes.float8_e4m3fn).view(np.uint8)
    else:
        c = by_word.astype(ml_dtypes.float4_e2m1fn).view(np.uint8) & 0xF
        words = (c[..., 0::2] | (c[..., 1::2] << 4)).reshape(k // 512, 128, 2 * n)
    return np.ascontiguousarray(words), np.ascontiguousarray(byte.astype(np.uint8).reshape(k // 512, 16, n))


def unpack_weight(words, scales, fmt):
    g, _, n = scales.shape
    words = np.ascontiguousarray(words).reshape(g, 128, n, -1)
    if fmt == "e4m3":
        vals = words.view(ml_dtypes.float8_e4m3fn).astype(np.float64)
    else:
        nib = np.empty((g, 128, n, 4), np.uint8)
        nib[..., 0::2] = words & 0xF
        nib[..., 1::2] = words >> 4
        vals = E2M1[nib]
    vals = vals * np.repeat(np.exp2(scales.astype(np.float64) - 127.0), 8, axis=1)[..., None]
    return vals.transpose(0, 1, 3, 2).reshape(g * 512, n)


def bf(x):
    return np.asarray(x, np.float32).astype(ml_dtypes.bfloat16)


def planes(Y):
    r, m = Y.shape
    b = f64(bf(Y)).reshape(r // 32, 32, m)
    amax = np.abs(b).max(1)
    byte = np.clip(np.where(amax > 0, np.frexp(amax)[1] - 1 + 127 - 7, 1), 1, 254)
    codes = (b * np.exp2(127.0 - byte)[:, None, :]).reshape(r, m).astype(np.float32).astype(ml_dtypes.float8_e4m3fn).view(np.uint8)
    words = codes.reshape(r // 512, 128, 4, m).transpose(0, 1, 3, 2)
    return np.ascontiguousarray(words), np.ascontiguousarray(byte.astype(np.uint8).reshape(r // 512, 16, m))


K, R, F, T, J, U = 512, 512, 512, 2048, 256, 512


def setup_inputs():
    n = np.random.standard_normal
    idx = np.random.permutation(T)[:J]
    idx2 = np.stack([np.random.permutation(U)[:J] for _ in range(8)])
    fk = mx_kscale(K)
    fr = mx_kscale(R)
    tabp = pack_weight(n((K, T)) / fk[:, None], "e2m1")
    dtabp = pack_weight(n((K, T)) / fk[:, None], "e2m1")
    return {
        "tab_words": tabp[0],
        "tab_scales": tabp[1],
        "dtab_words": dtabp[0],
        "dtab_scales": dtabp[1],
        "w1": (n((K, R)) * 1 / np.sqrt(K) * fk[:, None]).astype(np.float32),
        "gain": (np.random.uniform(0.5, 1.5, (R, 1))).astype(np.float32),
        "ground": (n((R, U)) * 0.7).astype(np.float32),
        "rs": (np.random.uniform(0.5, 2.0, (R, 1)) * fr[:, None]).astype(np.float32),
        "wor": (n((R, F)) * 1 / np.sqrt(R) / fr[:, None]).astype(np.float32),
        "res": (n((F, U)) * 0.5).astype(np.float32),
        "offs": striped(idx),
        "offs2": striped8(idx2),
    }


def reference(tab_words, tab_scales, dtab_words, dtab_scales, w1, gain, ground, rs, wor, res, offs, offs2):
    idx = unstriped(offs)
    idx2 = unstriped8(offs2)
    tabu = unpack_weight(tab_words, tab_scales, "e2m1")
    dtabu = unpack_weight(dtab_words, dtab_scales, "e2m1")
    w1q = mxq(f64(w1), 0, "e4m3")
    tabidxg = tabu[:, idx]
    a = w1q.T @ tabidxg
    dtabidxg = dtabu[:, idx]
    ta = w1q.T @ dtabidxg
    h1 = a * f64(gain)
    pg = np.zeros((R, U))
    pg[np.arange(R)[:, None], idx2[np.arange(R) % 512 // 64]] = h1
    s = pg + f64(ground)
    u1 = np.tanh(s)
    th1 = ta * f64(gain)
    tpg = np.zeros((R, U))
    tpg[np.arange(R)[:, None], idx2[np.arange(R) % 512 // 64]] = th1
    ts = tpg
    tu1 = ts * (1.0 - np.square(u1))
    fo1 = tu1 * f64(rs)
    worq = mxq(f64(wor), 0, "e4m3")
    fo1q = mxq(fo1, 0, "e4m3")
    yo = worq.T @ fo1q
    y = yo + f64(res)
    words, scales = planes(y)
    return y, words, scales

@@ -1,0 +1,194 @@
+from contextlib import ExitStack
+
+import concourse.mybir as mybir
+
+F32 = mybir.dt.float32
+BF16 = mybir.dt.bfloat16
+I32 = mybir.dt.int32
+U32 = mybir.dt.uint32
+U16 = mybir.dt.uint16
+U8 = mybir.dt.uint8
+FP8X4 = mybir.dt.float8_e4m3fn_x4
+FP4X4 = mybir.dt.float4_e2m1fn_x4
+ACT = mybir.ActivationFunctionType
+ALU = mybir.AluOpType
+
+P = 128
+PACK = 4
+K, R, F, T, J, U = 512, 512, 512, 2048, 256, 512
+CH = 128
+NCH = U // CH
+NWIN = 2
+FLOPS = 2 * K * R * J * 2 + 2 * R * F * U
+
+
+def tile_attend_tcpageput_o_pl_kernel(tc, tab_words, tab_scales, dtab_words, dtab_scales, w1, gain, ground, rs, wor, res, offs, offs2, out_0, out_1, out_2):
+    nc = tc.nc
+    with ExitStack() as ctx:
+        sb = ctx.enter_context(tc.tile_pool(name="sb", bufs=1))
+        ps = ctx.enter_context(tc.psum_pool(name="ps", bufs=8))
+
+        def tile(name, shape, dtype, tag=None):
+            return sb.tile(shape, dtype, name=name, tag=tag or name, align_bytes=64)
+
+        def bank(name):
+            return ps.tile([P, 512], F32, name=name, tag="bank")
+
+        tab_s = tile("tab_s", [P, T], U8)
+        nc.gpsimd.memset(tab_s[:].bitcast(I32), 0)
+        wins = [tile("win%d" % t, [P, U], F32) for t in range(NWIN)]
+        for t in range(NWIN):
+            nc.vector.memset(wins[t][:], 0.0)
+        page = [wins[t % NWIN] for t in range(PACK)]
+        tpage = [wins[(PACK + t) % NWIN] for t in range(PACK)]
+        warm = tile("warm", [P, 8], F32)
+        nc.scalar.activation(warm[:, 0:1], page[0][:, 0:1], ACT.Tanh)
+
+        def load_scales(eng, dst, src):
+            for q in range(4):
+                eng.dma_start(out=dst[32 * q : 32 * q + 4, :].bitcast(I32), in_=src[0, 4 * q : 4 * q + 4, :].bitcast(I32))
+
+        w1v = w1.rearrange("(p j) c -> p j c", j=PACK)
+        w1raw = [tile("w1raw%d" % h, [P, PACK, R // 2], F32) for h in range(2)]
+        o1 = sb.tile([P, J // 16], U16, name="o1")
+        o2 = sb.tile([P, J // 16], U16, name="o2")
+        tab_w = tile("tab_w", [P, T], U16)
+        gain_t = tile("gain_t", [P, PACK], F32)
+        rs_t = tile("rs_t", [P, PACK], F32)
+        nc.sync.dma_start(o1[:], offs)
+        nc.sync.dma_start(out=w1raw[0][:], in_=w1v[:, :, 0 : R // 2])
+        nc.sync.dma_start(out=w1raw[1][:], in_=w1v[:, :, R // 2 : R])
+        nc.sync.dma_start(out=tab_w[:].bitcast(I32), in_=tab_words[0].bitcast(I32))
+        load_scales(nc.scalar, tab_s, tab_scales)
+        nc.gpsimd.dma_start(out=gain_t[:], in_=gain.rearrange("(p t) o -> p (t o)", t=PACK))
+        nc.gpsimd.dma_start(out=rs_t[:], in_=rs.rearrange("(p t) o -> p (t o)", t=PACK))
+        nc.sync.dma_start(o2[:], offs2)
+
+        def deal(copy, dst, src, m0, s0, n):
+            copy(dst[:, :, m0 : m0 + n, :].rearrange("p t m j -> p m j t"),
+                 src[:, :, PACK * s0 : PACK * (s0 + n)].rearrange("p j (m t) -> p m j t", t=PACK))
+
+        w1b = tile("w1b", [P, PACK, P, PACK], BF16)
+        deal(nc.vector.tensor_copy, w1b, w1raw[0], 0, 0, 64)
+        g_s = tile("g_s", [P, J], U8)
+        g_w = tile("g_w", [P, J], U16)
+        dg_s = tile("dg_s", [P, J], U8)
+        dg_w = tile("dg_w", [P, J], U16)
+        nc.vector.tensor_copy(g_s[:], tab_s[:].indirect(o1[:]))
+        deal(nc.vector.tensor_copy, w1b, w1raw[1], 64, 0, 40)
+        deal(nc.scalar.copy, w1b, w1raw[1], 104, 40, 24)
+        w1c = tile("w1c", [P, R], U32)
+        w1s = tile("w1s", [P, R], U8)
+
+        def quant(codes, scales, src):
+            nc.vector.quantize_mx(out=codes.bitcast(FP8X4), scales=scales, in_=src)
+
+        w1flat = w1b[:].rearrange("p t m j -> p (t m j)")
+        quant(w1c[:, 0:128], w1s[:, 0:128], w1flat[:, 0:512])
+        nc.vector.tensor_copy(g_w[:], tab_w[:].indirect(o1[:]))
+        quant(w1c[:, 128:256], w1s[:, 128:256], w1flat[:, 512:1024])
+        quant(w1c[:, 256:512], w1s[:, 256:512], w1flat[:, 1024:2048])
+
+        ground_t = tile("ground_t", [P, PACK, U], F32, tag="w1raw0")
+        nc.sync.dma_start(out=ground_t[:], in_=ground.rearrange("(p t) u -> p t u", t=PACK))
+        dtab_s = tile("dtab_s", [P, T], U8, tag="tab_s")
+        nc.gpsimd.memset(dtab_s[:].bitcast(I32), 0)
+        load_scales(nc.sync, dtab_s, dtab_scales)
+        dtab_w = tile("dtab_w", [P, T], U16, tag="w1raw1")
+        nc.sync.dma_start(out=dtab_w[:].bitcast(I32), in_=dtab_words[0].bitcast(I32))
+        wor_raw = tile("wor_raw", [P, PACK, F], F32, tag="tab_w")
+        nc.sync.dma_start(out=wor_raw[:], in_=wor.rearrange("(p j) c -> p j c", j=PACK))
+        res_t = tile("res_t", [P, PACK, U], F32, tag="w1b")
+        nc.sync.dma_start(out=res_t[:], in_=res.rearrange("(p t) u -> p t u", t=PACK))
+
+        def first_layer(name, words, scales, t):
+            acc = bank(name + "acc%d" % t)
+            nc.tensor.matmul_mx(out=acc[:, 0:J], lhsT=w1c[:, P * t : P * (t + 1)].bitcast(FP8X4), lhsT_scale=w1s[:, P * t : P * (t + 1)],
+                                rhs=words[:].bitcast(FP4X4), rhs_scale=scales[:], start=True, stop=True)
+            h = tile(name + "%d" % t, [P, J], F32)
+            nc.scalar.activation(h[:], acc[:, 0:J], ACT.Copy, scale=gain_t[:, t : t + 1])
+            return h
+
+        h1 = [first_layer("h1_", g_w, g_s, t) for t in range(PACK)]
+        nrs_t = tile("nrs_t", [P, PACK], F32)
+        nc.scalar.activation(nrs_t[:], rs_t[:], ACT.Copy, scale=-1.0)
+
+        worb = tile("worb", [P, PACK, P, PACK], BF16)
+        slope = []
+        th1 = []
+        for t in range(PACK):
+            nc.vector.tensor_copy(page[t][:].indirect(o2[:]), h1[t][:])
+            st = tile("s%d" % t, [P, U], F32)
+            nc.gpsimd.tensor_tensor(st[:], page[t][:], ground_t[:, t, :], ALU.add)
+            if t == 3:
+                for g in range(4):
+                    deal(nc.scalar.copy, worb, wor_raw, 32 * g, 32 * g, 32)
+            ut = tile("u%d" % t, [P, U], F32)
+            nc.scalar.activation(ut[:], st[:], ACT.Tanh)
+            vt = tile("v%d" % t, [P, U], F32)
+            nc.scalar.activation(vt[:], ut[:], ACT.Square)
+            sl = tile("slope%d" % t, [P, U], F32)
+            nc.scalar.activation(sl[:], vt[:], ACT.Identity, scale=nrs_t[:, t : t + 1], bias=rs_t[:, t : t + 1])
+            slope.append(sl)
+            if t == 1:
+                nc.vector.tensor_copy(dg_s[:], dtab_s[:].indirect(o1[:]))
+                nc.vector.tensor_copy(dg_w[:], dtab_w[:].indirect(o1[:]))
+                th1 = [first_layer("th1_", dg_w, dg_s, i) for i in range(PACK)]
+
+        worc = tile("worc", [P, F], U32)
+        wors = tile("wors", [P, F], U8)
+
+        fo = tile("fo", [P, PACK, U], BF16)
+        for t in range(PACK):
+            nc.vector.tensor_copy(tpage[t][:].indirect(o2[:]), th1[t][:])
+            if t < PACK - 1:
+                nc.gpsimd.tensor_tensor(fo[:, t, :], tpage[t][:], slope[t][:], ALU.mult)
+            if t == 2:
+                quant(worc[:], wors[:], worb[:].rearrange("p t m j -> p (t m j)"))
+        last = PACK - 1
+        nc.vector.tensor_tensor(fo[:, last, 0:CH], tpage[last][:, 0:CH], slope[last][:, 0:CH], ALU.mult)
+        nc.vector.tensor_tensor(fo[:, last, CH:U], tpage[last][:, CH:U], slope[last][:, CH:U], ALU.mult)
+
+        def weave(copy, dst, src):
+            copy(dst.rearrange("p (c i) t -> p c t i", i=4), src.rearrange("p t (c i) -> p c t i", i=4))
+
+        foc = [tile("foc%d" % c, [P, CH], U32) for c in range(NCH)]
+        fos = [tile("fos%d" % c, [P, CH], U8) for c in range(NCH)]
+        accs = []
+        for c in range(NCH):
+            cols = slice(CH * c, CH * (c + 1))
+            fw = tile("fw%d" % c, [P, CH, PACK], BF16)
+            weave(nc.scalar.copy if c % 2 == 0 else nc.vector.tensor_copy, fw[:], fo[:, :, cols])
+            quant(foc[c][:], fos[c][:], fw[:].rearrange("p u t -> p (u t)"))
+            acc = bank("yacc%d" % c)
+            for t in range(PACK):
+                nc.tensor.matmul_mx(out=acc[:, CH * t : CH * (t + 1)], lhsT=worc[:, P * t : P * (t + 1)].bitcast(FP8X4), lhsT_scale=wors[:, P * t : P * (t + 1)],
+                                    rhs=foc[c][:].bitcast(FP8X4), rhs_scale=fos[c][:], start=True, stop=True)
+            accs.append(acc)
+
+        y = tile("y", [P, PACK, U], F32)
+        yc = tile("yc", [P, U], U32)
+        ys = tile("ys", [P, U], U8)
+        outv = out_0.rearrange("(p t) u -> p t u", t=PACK)
+        wordv = out_1[0].rearrange("p c r -> p (c r)").bitcast(I32)
+        yws = []
+        for c in range(NCH + 1):
+            if c < NCH:
+                cols = slice(CH * c, CH * (c + 1))
+                nc.vector.tensor_tensor(y[:, :, cols], accs[c][:].rearrange("p (t u) -> p t u", t=PACK), res_t[:, :, cols], ALU.add)
+                yw = tile("yw%d" % c, [P, CH, PACK], BF16)
+                weave(nc.scalar.copy, yw[:], y[:, :, cols])
+                yws.append(yw)
+                if c == 1:
+                    nc.sync.dma_start(out=outv[:, :, 0 : 2 * CH], in_=y[:, :, 0 : 2 * CH])
+                if c > 1:
+                    nc.sync.dma_start(out=outv[:, :, cols], in_=y[:, :, cols])
+            if c > 0:
+                pc = slice(CH * (c - 1), CH * c)
+                quant(yc[:, pc], ys[:, pc], yws[c - 1][:].rearrange("p u t -> p (u t)"))
+                if c == NCH - 1:
+                    nc.sync.dma_start(out=wordv[:, 0 : CH * c], in_=yc[:, 0 : CH * c].bitcast(I32))
+        nc.sync.dma_start(out=wordv[:, U - CH : U], in_=yc[:, U - CH : U].bitcast(I32))
+        for q in range(4):
+            eng = nc.scalar if q < 2 else nc.sync
+            eng.dma_start(out=out_2[0, 4 * q : 4 * q + 4, :].bitcast(I32), in_=ys[32 * q : 32 * q + 4, :].bitcast(I32))

@@ -1,6 +1,7 @@
 from contextlib import ExitStack
 
 import concourse.mybir as mybir
+from concourse.masks import make_identity
 
 F32 = mybir.dt.float32
 BF16 = mybir.dt.bfloat16
@@ -18,7 +19,7 @@ PACK = 4
 K, R, F, T, J, U = 512, 512, 512, 2048, 256, 512
 CH = 128
 NCH = U // CH
-NWIN = 2
+NWIN = 3
 FLOPS = 2 * K * R * J * 2 + 2 * R * F * U
 
 
@@ -26,16 +27,18 @@ def tile_attend_tcpageput_o_pl_kernel(tc, tab_words, tab_scales, dtab_words, dta
     nc = tc.nc
     with ExitStack() as ctx:
         sb = ctx.enter_context(tc.tile_pool(name="sb", bufs=1))
-        ps = ctx.enter_context(tc.psum_pool(name="ps", bufs=8))
+        ps = ctx.enter_context(tc.psum_pool(name="ps", bufs=1))
 
-        def tile(name, shape, dtype, tag=None):
-            return sb.tile(shape, dtype, name=name, tag=tag or name, align_bytes=64)
+        def tile(name, shape, dtype):
+            return sb.tile(shape, dtype, name=name, align_bytes=64)
 
-        def bank(name):
-            return ps.tile([P, 512], F32, name=name, tag="bank")
+        def bank(name, b):
+            return ps.tile([P, 512], F32, name=name, tag="bank%d" % b)
 
         tab_s = tile("tab_s", [P, T], U8)
+        dtab_s = tile("dtab_s", [P, T], U8)
         nc.gpsimd.memset(tab_s[:].bitcast(I32), 0)
+        nc.gpsimd.memset(dtab_s[:].bitcast(I32), 0)
         wins = [tile("win%d" % t, [P, U], F32) for t in range(NWIN)]
         for t in range(NWIN):
             nc.vector.memset(wins[t][:], 0.0)
@@ -53,28 +56,40 @@ def tile_attend_tcpageput_o_pl_kernel(tc, tab_words, tab_scales, dtab_words, dta
         o1 = sb.tile([P, J // 16], U16, name="o1")
         o2 = sb.tile([P, J // 16], U16, name="o2")
         tab_w = tile("tab_w", [P, T], U16)
+        dtab_w = tile("dtab_w", [P, T], U16)
         gain_t = tile("gain_t", [P, PACK], F32)
         rs_t = tile("rs_t", [P, PACK], F32)
+        ground_t = tile("ground_t", [P, PACK, U], F32)
+        wor_raw = tile("wor_raw", [P, PACK, F], F32)
+        res_t = tile("res_t", [P, PACK, U], F32)
+        ident = tile("ident", [P, P], F32)
         nc.sync.dma_start(o1[:], offs)
+        nc.sync.dma_start(out=tab_w[:].bitcast(I32), in_=tab_words[0].bitcast(I32))
         nc.sync.dma_start(out=w1raw[0][:], in_=w1v[:, :, 0 : R // 2])
         nc.sync.dma_start(out=w1raw[1][:], in_=w1v[:, :, R // 2 : R])
-        nc.sync.dma_start(out=tab_w[:].bitcast(I32), in_=tab_words[0].bitcast(I32))
         load_scales(nc.scalar, tab_s, tab_scales)
         nc.gpsimd.dma_start(out=gain_t[:], in_=gain.rearrange("(p t) o -> p (t o)", t=PACK))
         nc.gpsimd.dma_start(out=rs_t[:], in_=rs.rearrange("(p t) o -> p (t o)", t=PACK))
+        make_identity(nc, ident[:])
+        nc.sync.dma_start(out=dtab_w[:].bitcast(I32), in_=dtab_words[0].bitcast(I32))
         nc.sync.dma_start(o2[:], offs2)
+        nc.sync.dma_start(out=ground_t[:], in_=ground.rearrange("(p t) u -> p t u", t=PACK))
+        load_scales(nc.sync, dtab_s, dtab_scales)
+        nc.sync.dma_start(out=wor_raw[:], in_=wor.rearrange("(p j) c -> p j c", j=PACK))
+        nc.sync.dma_start(out=res_t[:], in_=res.rearrange("(p t) u -> p t u", t=PACK))
 
         def deal(copy, dst, src, m0, s0, n):
             copy(dst[:, :, m0 : m0 + n, :].rearrange("p t m j -> p m j t"),
                  src[:, :, PACK * s0 : PACK * (s0 + n)].rearrange("p j (m t) -> p m j t", t=PACK))
 
         w1b = tile("w1b", [P, PACK, P, PACK], BF16)
-        deal(nc.vector.tensor_copy, w1b, w1raw[0], 0, 0, 64)
         g_s = tile("g_s", [P, J], U8)
         g_w = tile("g_w", [P, J], U16)
         dg_s = tile("dg_s", [P, J], U8)
         dg_w = tile("dg_w", [P, J], U16)
+        nc.vector.tensor_copy(g_w[:], tab_w[:].indirect(o1[:]))
         nc.vector.tensor_copy(g_s[:], tab_s[:].indirect(o1[:]))
+        deal(nc.vector.tensor_copy, w1b, w1raw[0], 0, 0, 64)
         deal(nc.vector.tensor_copy, w1b, w1raw[1], 64, 0, 40)
         deal(nc.scalar.copy, w1b, w1raw[1], 104, 40, 24)
         w1c = tile("w1c", [P, R], U32)
@@ -85,31 +100,25 @@ def tile_attend_tcpageput_o_pl_kernel(tc, tab_words, tab_scales, dtab_words, dta
 
         w1flat = w1b[:].rearrange("p t m j -> p (t m j)")
         quant(w1c[:, 0:128], w1s[:, 0:128], w1flat[:, 0:512])
-        nc.vector.tensor_copy(g_w[:], tab_w[:].indirect(o1[:]))
         quant(w1c[:, 128:256], w1s[:, 128:256], w1flat[:, 512:1024])
         quant(w1c[:, 256:512], w1s[:, 256:512], w1flat[:, 1024:2048])
 
-        ground_t = tile("ground_t", [P, PACK, U], F32, tag="w1raw0")
-        nc.sync.dma_start(out=ground_t[:], in_=ground.rearrange("(p t) u -> p t u", t=PACK))
-        dtab_s = tile("dtab_s", [P, T], U8, tag="tab_s")
-        nc.gpsimd.memset(dtab_s[:].bitcast(I32), 0)
-        load_scales(nc.sync, dtab_s, dtab_scales)
-        dtab_w = tile("dtab_w", [P, T], U16, tag="w1raw1")
-        nc.sync.dma_start(out=dtab_w[:].bitcast(I32), in_=dtab_words[0].bitcast(I32))
-        wor_raw = tile("wor_raw", [P, PACK, F], F32, tag="tab_w")
-        nc.sync.dma_start(out=wor_raw[:], in_=wor.rearrange("(p j) c -> p j c", j=PACK))
-        res_t = tile("res_t", [P, PACK, U], F32, tag="w1b")
-        nc.sync.dma_start(out=res_t[:], in_=res.rearrange("(p t) u -> p t u", t=PACK))
-
-        def first_layer(name, words, scales, t):
-            acc = bank(name + "acc%d" % t)
-            nc.tensor.matmul_mx(out=acc[:, 0:J], lhsT=w1c[:, P * t : P * (t + 1)].bitcast(FP8X4), lhsT_scale=w1s[:, P * t : P * (t + 1)],
+        def first_mm(acc, words, scales, t):
+            nc.tensor.matmul_mx(out=acc, lhsT=w1c[:, P * t : P * (t + 1)].bitcast(FP8X4), lhsT_scale=w1s[:, P * t : P * (t + 1)],
                                 rhs=words[:].bitcast(FP4X4), rhs_scale=scales[:], start=True, stop=True)
+
+        def times_gain(name, acc, t):
             h = tile(name + "%d" % t, [P, J], F32)
-            nc.scalar.activation(h[:], acc[:, 0:J], ACT.Copy, scale=gain_t[:, t : t + 1])
+            nc.scalar.activation(h[:], acc, ACT.Copy, scale=gain_t[:, t : t + 1])
             return h
 
-        h1 = [first_layer("h1_", g_w, g_s, t) for t in range(PACK)]
+        h1 = []
+        for t in range(PACK):
+            acc = bank("a%d" % t, t)
+            first_mm(acc[:, 0:J], g_w, g_s, t)
+            h1.append(times_gain("h1_", acc[:, 0:J], t))
+        nc.vector.tensor_copy(dg_w[:], dtab_w[:].indirect(o1[:]))
+        nc.vector.tensor_copy(dg_s[:], dtab_s[:].indirect(o1[:]))
         nrs_t = tile("nrs_t", [P, PACK], F32)
         nc.scalar.activation(nrs_t[:], rs_t[:], ACT.Copy, scale=-1.0)
 
@@ -118,22 +127,33 @@ def tile_attend_tcpageput_o_pl_kernel(tc, tab_words, tab_scales, dtab_words, dta
         th1 = []
         for t in range(PACK):
             nc.vector.tensor_copy(page[t][:].indirect(o2[:]), h1[t][:])
-            st = tile("s%d" % t, [P, U], F32)
-            nc.gpsimd.tensor_tensor(st[:], page[t][:], ground_t[:, t, :], ALU.add)
+            sT = bank("sT%d" % t, PACK + t)
+            for c in range(NCH):
+                cols = slice(CH * c, CH * (c + 1))
+                nc.tensor.matmul(sT[:, cols], ground_t[:, t, cols], ident[:], start=(c == 0), stop=False, is_transpose=True)
+            for c in range(NCH):
+                cols = slice(CH * c, CH * (c + 1))
+                nc.tensor.matmul(sT[:, cols], page[t][:, cols], ident[:], start=False, stop=(c == NCH - 1), is_transpose=True)
             if t == 3:
                 for g in range(4):
                     deal(nc.scalar.copy, worb, wor_raw, 32 * g, 32 * g, 32)
-            ut = tile("u%d" % t, [P, U], F32)
-            nc.scalar.activation(ut[:], st[:], ACT.Tanh)
-            vt = tile("v%d" % t, [P, U], F32)
-            nc.scalar.activation(vt[:], ut[:], ACT.Square)
+            uT = tile("uT%d" % t, [P, U], F32)
+            nc.scalar.activation(uT[:], sT[:], ACT.Tanh)
+            if t < 2:
+                acc = bank("ta%d" % t, PACK + t)
+                for i in range(2):
+                    first_mm(acc[:, J * i : J * (i + 1)], dg_w, dg_s, 2 * t + i)
+                for i in range(2):
+                    th1.append(times_gain("th1_", acc[:, J * i : J * (i + 1)], 2 * t + i))
+            vT = tile("vT%d" % t, [P, U], F32)
+            nc.scalar.activation(vT[:], uT[:], ACT.Square)
+            vb = bank("vb%d" % t, t)
+            for c in range(NCH):
+                cols = slice(CH * c, CH * (c + 1))
+                nc.tensor.transpose(vb[:, cols], vT[:, cols], ident[:])
             sl = tile("slope%d" % t, [P, U], F32)
-            nc.scalar.activation(sl[:], vt[:], ACT.Identity, scale=nrs_t[:, t : t + 1], bias=rs_t[:, t : t + 1])
+            nc.scalar.activation(sl[:], vb[:], ACT.Identity, scale=nrs_t[:, t : t + 1], bias=rs_t[:, t : t + 1])
             slope.append(sl)
-            if t == 1:
-                nc.vector.tensor_copy(dg_s[:], dtab_s[:].indirect(o1[:]))
-                nc.vector.tensor_copy(dg_w[:], dtab_w[:].indirect(o1[:]))
-                th1 = [first_layer("th1_", dg_w, dg_s, i) for i in range(PACK)]
 
         worc = tile("worc", [P, F], U32)
         wors = tile("wors", [P, F], U8)
@@ -141,8 +161,8 @@ def tile_attend_tcpageput_o_pl_kernel(tc, tab_words, tab_scales, dtab_words, dta
         fo = tile("fo", [P, PACK, U], BF16)
         for t in range(PACK):
             nc.vector.tensor_copy(tpage[t][:].indirect(o2[:]), th1[t][:])
-            if t < PACK - 1:
-                nc.gpsimd.tensor_tensor(fo[:, t, :], tpage[t][:], slope[t][:], ALU.mult)
+            if t > 0:
+                nc.vector.tensor_tensor(fo[:, t - 1, :], tpage[t - 1][:], slope[t - 1][:], ALU.mult)
             if t == 2:
                 quant(worc[:], wors[:], worb[:].rearrange("p t m j -> p (t m j)"))
         last = PACK - 1
@@ -158,9 +178,9 @@ def tile_attend_tcpageput_o_pl_kernel(tc, tab_words, tab_scales, dtab_words, dta
         for c in range(NCH):
             cols = slice(CH * c, CH * (c + 1))
             fw = tile("fw%d" % c, [P, CH, PACK], BF16)
-            weave(nc.scalar.copy if c % 2 == 0 else nc.vector.tensor_copy, fw[:], fo[:, :, cols])
+            weave(nc.vector.tensor_copy if c == 1 else nc.scalar.copy, fw[:], fo[:, :, cols])
             quant(foc[c][:], fos[c][:], fw[:].rearrange("p u t -> p (u t)"))
-            acc = bank("yacc%d" % c)
+            acc = bank("yacc%d" % c, PACK + (c + 2) % PACK)
             for t in range(PACK):
                 nc.tensor.matmul_mx(out=acc[:, CH * t : CH * (t + 1)], lhsT=worc[:, P * t : P * (t + 1)].bitcast(FP8X4), lhsT_scale=wors[:, P * t : P * (t + 1)],
                                     rhs=foc[c][:].bitcast(FP8X4), rhs_scale=fos[c][:], start=True, stop=True)

@@ -1,7 +1,6 @@
 from contextlib import ExitStack
 
 import concourse.mybir as mybir
-from concourse.masks import make_identity
 
 F32 = mybir.dt.float32
 BF16 = mybir.dt.bfloat16
@@ -29,8 +28,8 @@ def tile_attend_tcpageput_o_pl_kernel(tc, tab_words, tab_scales, dtab_words, dta
         sb = ctx.enter_context(tc.tile_pool(name="sb", bufs=1))
         ps = ctx.enter_context(tc.psum_pool(name="ps", bufs=1))
 
-        def tile(name, shape, dtype):
-            return sb.tile(shape, dtype, name=name, align_bytes=64)
+        def tile(name, shape, dtype, tag=None):
+            return sb.tile(shape, dtype, name=name, tag=tag or name, align_bytes=64)
 
         def bank(name, b):
             return ps.tile([P, 512], F32, name=name, tag="bank%d" % b)
@@ -62,7 +61,6 @@ def tile_attend_tcpageput_o_pl_kernel(tc, tab_words, tab_scales, dtab_words, dta
         ground_t = tile("ground_t", [P, PACK, U], F32)
         wor_raw = tile("wor_raw", [P, PACK, F], F32)
         res_t = tile("res_t", [P, PACK, U], F32)
-        ident = tile("ident", [P, P], F32)
         nc.sync.dma_start(o1[:], offs)
         nc.sync.dma_start(out=tab_w[:].bitcast(I32), in_=tab_words[0].bitcast(I32))
         nc.sync.dma_start(out=w1raw[0][:], in_=w1v[:, :, 0 : R // 2])
@@ -70,7 +68,6 @@ def tile_attend_tcpageput_o_pl_kernel(tc, tab_words, tab_scales, dtab_words, dta
         load_scales(nc.scalar, tab_s, tab_scales)
         nc.gpsimd.dma_start(out=gain_t[:], in_=gain.rearrange("(p t) o -> p (t o)", t=PACK))
         nc.gpsimd.dma_start(out=rs_t[:], in_=rs.rearrange("(p t) o -> p (t o)", t=PACK))
-        make_identity(nc, ident[:])
         nc.sync.dma_start(out=dtab_w[:].bitcast(I32), in_=dtab_words[0].bitcast(I32))
         nc.sync.dma_start(o2[:], offs2)
         nc.sync.dma_start(out=ground_t[:], in_=ground.rearrange("(p t) u -> p t u", t=PACK))
@@ -107,8 +104,8 @@ def tile_attend_tcpageput_o_pl_kernel(tc, tab_words, tab_scales, dtab_words, dta
             nc.tensor.matmul_mx(out=acc, lhsT=w1c[:, P * t : P * (t + 1)].bitcast(FP8X4), lhsT_scale=w1s[:, P * t : P * (t + 1)],
                                 rhs=words[:].bitcast(FP4X4), rhs_scale=scales[:], start=True, stop=True)
 
-        def times_gain(name, acc, t):
-            h = tile(name + "%d" % t, [P, J], F32)
+        def times_gain(name, acc, t, tag=None):
+            h = tile(name + "%d" % t, [P, J], F32, tag=tag)
             nc.scalar.activation(h[:], acc, ACT.Copy, scale=gain_t[:, t : t + 1])
             return h
 
@@ -119,41 +116,35 @@ def tile_attend_tcpageput_o_pl_kernel(tc, tab_words, tab_scales, dtab_words, dta
             h1.append(times_gain("h1_", acc[:, 0:J], t))
         nc.vector.tensor_copy(dg_w[:], dtab_w[:].indirect(o1[:]))
         nc.vector.tensor_copy(dg_s[:], dtab_s[:].indirect(o1[:]))
+        th1 = []
+        ta = []
+        for t in range(PACK):
+            acc = bank("ta%d" % t, PACK + t)
+            first_mm(acc[:, 0:J], dg_w, dg_s, t)
+            ta.append(acc)
         nrs_t = tile("nrs_t", [P, PACK], F32)
-        nc.scalar.activation(nrs_t[:], rs_t[:], ACT.Copy, scale=-1.0)
+        nc.gpsimd.tensor_scalar(nrs_t[:], rs_t[:], -1.0, 0.0, ALU.mult, ALU.add)
 
         worb = tile("worb", [P, PACK, P, PACK], BF16)
         slope = []
-        th1 = []
         for t in range(PACK):
             nc.vector.tensor_copy(page[t][:].indirect(o2[:]), h1[t][:])
-            sT = bank("sT%d" % t, PACK + t)
-            for c in range(NCH):
-                cols = slice(CH * c, CH * (c + 1))
-                nc.tensor.matmul(sT[:, cols], ground_t[:, t, cols], ident[:], start=(c == 0), stop=False, is_transpose=True)
-            for c in range(NCH):
-                cols = slice(CH * c, CH * (c + 1))
-                nc.tensor.matmul(sT[:, cols], page[t][:, cols], ident[:], start=False, stop=(c == NCH - 1), is_transpose=True)
+            st = tile("s%d" % t, [P, U], F32)
+            nc.gpsimd.tensor_tensor(st[:], page[t][:], ground_t[:, t, :], ALU.add)
             if t == 3:
                 for g in range(4):
                     deal(nc.scalar.copy, worb, wor_raw, 32 * g, 32 * g, 32)
-            uT = tile("uT%d" % t, [P, U], F32)
-            nc.scalar.activation(uT[:], sT[:], ACT.Tanh)
-            if t < 2:
-                acc = bank("ta%d" % t, PACK + t)
-                for i in range(2):
-                    first_mm(acc[:, J * i : J * (i + 1)], dg_w, dg_s, 2 * t + i)
-                for i in range(2):
-                    th1.append(times_gain("th1_", acc[:, J * i : J * (i + 1)], 2 * t + i))
-            vT = tile("vT%d" % t, [P, U], F32)
-            nc.scalar.activation(vT[:], uT[:], ACT.Square)
-            vb = bank("vb%d" % t, t)
-            for c in range(NCH):
-                cols = slice(CH * c, CH * (c + 1))
-                nc.tensor.transpose(vb[:, cols], vT[:, cols], ident[:])
+            ut = tile("u%d" % t, [P, U], F32)
+            nc.scalar.activation(ut[:], st[:], ACT.Tanh)
+            vt = tile("v%d" % t, [P, U], F32)
+            nc.scalar.activation(vt[:], ut[:], ACT.Square)
+            if t in (1, 2):
+                th1.append(times_gain("th1_", ta[2 * t - 2][:, 0:J], 2 * t - 2, tag="u%d" % t))
             sl = tile("slope%d" % t, [P, U], F32)
-            nc.scalar.activation(sl[:], vb[:], ACT.Identity, scale=nrs_t[:, t : t + 1], bias=rs_t[:, t : t + 1])
+            nc.scalar.activation(sl[:], vt[:], ACT.Identity, scale=nrs_t[:, t : t + 1], bias=rs_t[:, t : t + 1])
             slope.append(sl)
+            if t in (1, 2):
+                th1.append(times_gain("th1_", ta[2 * t - 1][:, 0:J], 2 * t - 1, tag="v%d" % t))
 
         worc = tile("worc", [P, F], U32)
         wors = tile("wors", [P, F], U8)
@@ -161,8 +152,8 @@ def tile_attend_tcpageput_o_pl_kernel(tc, tab_words, tab_scales, dtab_words, dta
         fo = tile("fo", [P, PACK, U], BF16)
         for t in range(PACK):
             nc.vector.tensor_copy(tpage[t][:].indirect(o2[:]), th1[t][:])
-            if t > 0:
-                nc.vector.tensor_tensor(fo[:, t - 1, :], tpage[t - 1][:], slope[t - 1][:], ALU.mult)
+            if t < PACK - 1:
+                nc.gpsimd.tensor_tensor(fo[:, t, :], tpage[t][:], slope[t][:], ALU.mult)
             if t == 2:
                 quant(worc[:], wors[:], worb[:].rearrange("p t m j -> p (t m j)"))
         last = PACK - 1
@@ -180,7 +171,7 @@ def tile_attend_tcpageput_o_pl_kernel(tc, tab_words, tab_scales, dtab_words, dta
             fw = tile("fw%d" % c, [P, CH, PACK], BF16)
             weave(nc.vector.tensor_copy if c == 1 else nc.scalar.copy, fw[:], fo[:, :, cols])
             quant(foc[c][:], fos[c][:], fw[:].rearrange("p u t -> p (u t)"))
-            acc = bank("yacc%d" % c, PACK + (c + 2) % PACK)
+            acc = bank("yacc%d" % c, c)
             for t in range(PACK):
                 nc.tensor.matmul_mx(out=acc[:, CH * t : CH * (t + 1)], lhsT=worc[:, P * t : P * (t + 1)].bitcast(FP8X4), lhsT_scale=wors[:, P * t : P * (t + 1)],
                                     rhs=foc[c][:].bitcast(FP8X4), rhs_scale=fos[c][:], start=True, stop=True)
@@ -197,12 +188,14 @@ def tile_attend_tcpageput_o_pl_kernel(tc, tab_words, tab_scales, dtab_words, dta
                 cols = slice(CH * c, CH * (c + 1))
                 nc.vector.tensor_tensor(y[:, :, cols], accs[c][:].rearrange("p (t u) -> p t u", t=PACK), res_t[:, :, cols], ALU.add)
                 yw = tile("yw%d" % c, [P, CH, PACK], BF16)
-                weave(nc.scalar.copy, yw[:], y[:, :, cols])
+                if c < NCH - 1:
+                    weave(nc.scalar.copy, yw[:], y[:, :, cols])
+                else:
+                    weave(nc.scalar.copy, yw[:, 0 : CH // 2, :], y[:, :, U - CH : U - CH // 2])
+                    weave(nc.vector.tensor_copy, yw[:, CH // 2 : CH, :], y[:, :, U - CH // 2 : U])
                 yws.append(yw)
-                if c == 1:
-                    nc.sync.dma_start(out=outv[:, :, 0 : 2 * CH], in_=y[:, :, 0 : 2 * CH])
-                if c > 1:
-                    nc.sync.dma_start(out=outv[:, :, cols], in_=y[:, :, cols])
+                if c % 2 == 1:
+                    nc.sync.dma_start(out=outv[:, :, CH * (c - 1) : CH * (c + 1)], in_=y[:, :, CH * (c - 1) : CH * (c + 1)])
             if c > 0:
                 pc = slice(CH * (c - 1), CH * c)
                 quant(yc[:, pc], ys[:, pc], yws[c - 1][:].rearrange("p u t -> p (u t)"))

@@ -76,8 +76,12 @@ def tile_attend_tcpageput_o_pl_kernel(tc, tab_words, tab_scales, dtab_words, dta
         nc.sync.dma_start(out=res_t[:], in_=res.rearrange("(p t) u -> p t u", t=PACK))
 
         def deal(copy, dst, src, m0, s0, n):
-            copy(dst[:, :, m0 : m0 + n, :].rearrange("p t m j -> p m j t"),
-                 src[:, :, PACK * s0 : PACK * (s0 + n)].rearrange("p j (m t) -> p m j t", t=PACK))
+            copy(dst[:, :, m0 : m0 + n, :].rearrange("p (h e) m j -> p h m j e", e=2),
+                 src[:, :, PACK * s0 : PACK * (s0 + n)].rearrange("p j (m h e) -> p h m j e", h=2, e=2))
+
+        def deal_rows(copy, dst, src, m0, s0, n):
+            copy(dst[:, :, m0 : m0 + n, :],
+                 src[:, :, PACK * s0 : PACK * (s0 + n)].rearrange("p j (m t) -> p t m j", t=PACK))
 
         w1b = tile("w1b", [P, PACK, P, PACK], BF16)
         g_s = tile("g_s", [P, J], U8)
@@ -86,9 +90,10 @@ def tile_attend_tcpageput_o_pl_kernel(tc, tab_words, tab_scales, dtab_words, dta
         dg_w = tile("dg_w", [P, J], U16)
         nc.vector.tensor_copy(g_w[:], tab_w[:].indirect(o1[:]))
         nc.vector.tensor_copy(g_s[:], tab_s[:].indirect(o1[:]))
-        deal(nc.vector.tensor_copy, w1b, w1raw[0], 0, 0, 64)
-        deal(nc.vector.tensor_copy, w1b, w1raw[1], 64, 0, 40)
-        deal(nc.scalar.copy, w1b, w1raw[1], 104, 40, 24)
+        deal_rows(nc.vector.tensor_copy, w1b, w1raw[0], 0, 0, 32)
+        deal(nc.scalar.copy, w1b, w1raw[0], 32, 32, 32)
+        deal_rows(nc.vector.tensor_copy, w1b, w1raw[1], 64, 0, 32)
+        deal(nc.scalar.copy, w1b, w1raw[1], 96, 32, 32)
         w1c = tile("w1c", [P, R], U32)
         w1s = tile("w1s", [P, R], U8)
 

from contextlib import ExitStack

import concourse.mybir as mybir

F32 = mybir.dt.float32
BF16 = mybir.dt.bfloat16
I32 = mybir.dt.int32
U32 = mybir.dt.uint32
U16 = mybir.dt.uint16
U8 = mybir.dt.uint8
FP8X4 = mybir.dt.float8_e4m3fn_x4
FP4X4 = mybir.dt.float4_e2m1fn_x4
ACT = mybir.ActivationFunctionType
ALU = mybir.AluOpType

P = 128
PACK = 4
K, R, F, T, J, U = 512, 512, 512, 2048, 256, 512
CH = 128
NCH = U // CH
NWIN = 3
FLOPS = 2 * K * R * J * 2 + 2 * R * F * U


def tile_attend_tcpageput_o_pl_kernel(tc, tab_words, tab_scales, dtab_words, dtab_scales, w1, gain, ground, rs, wor, res, offs, offs2, out_0, out_1, out_2):
    nc = tc.nc
    with ExitStack() as ctx:
        sb = ctx.enter_context(tc.tile_pool(name="sb", bufs=1))
        ps = ctx.enter_context(tc.psum_pool(name="ps", bufs=1))

        def tile(name, shape, dtype, tag=None):
            return sb.tile(shape, dtype, name=name, tag=tag or name, align_bytes=64)

        def bank(name, b):
            return ps.tile([P, 512], F32, name=name, tag="bank%d" % b)

        tab_s = tile("tab_s", [P, T], U8)
        dtab_s = tile("dtab_s", [P, T], U8)
        nc.gpsimd.memset(tab_s[:].bitcast(I32), 0)
        nc.gpsimd.memset(dtab_s[:].bitcast(I32), 0)
        wins = [tile("win%d" % t, [P, U], F32) for t in range(NWIN)]
        for t in range(NWIN):
            nc.vector.memset(wins[t][:], 0.0)
        page = [wins[t % NWIN] for t in range(PACK)]
        tpage = [wins[(PACK + t) % NWIN] for t in range(PACK)]
        warm = tile("warm", [P, 8], F32)
        nc.scalar.activation(warm[:, 0:1], page[0][:, 0:1], ACT.Tanh)

        def load_scales(eng, dst, src):
            for q in range(4):
                eng.dma_start(out=dst[32 * q : 32 * q + 4, :].bitcast(I32), in_=src[0, 4 * q : 4 * q + 4, :].bitcast(I32))

        w1v = w1.rearrange("(p j) c -> p j c", j=PACK)
        w1raw = [tile("w1raw%d" % h, [P, PACK, R // 2], F32) for h in range(2)]
        o1 = sb.tile([P, J // 16], U16, name="o1")
        o2 = sb.tile([P, J // 16], U16, name="o2")
        tab_w = tile("tab_w", [P, T], U16)
        dtab_w = tile("dtab_w", [P, T], U16)
        gain_t = tile("gain_t", [P, PACK], F32)
        rs_t = tile("rs_t", [P, PACK], F32)
        ground_t = tile("ground_t", [P, PACK, U], F32)
        wor_raw = tile("wor_raw", [P, PACK, F], F32)
        res_t = tile("res_t", [P, PACK, U], F32)
        nc.sync.dma_start(o1[:], offs)
        nc.sync.dma_start(out=tab_w[:].bitcast(I32), in_=tab_words[0].bitcast(I32))
        nc.sync.dma_start(out=w1raw[0][:], in_=w1v[:, :, 0 : R // 2])
        nc.sync.dma_start(out=w1raw[1][:], in_=w1v[:, :, R // 2 : R])
        load_scales(nc.scalar, tab_s, tab_scales)
        nc.gpsimd.dma_start(out=gain_t[:], in_=gain.rearrange("(p t) o -> p (t o)", t=PACK))
        nc.gpsimd.dma_start(out=rs_t[:], in_=rs.rearrange("(p t) o -> p (t o)", t=PACK))
        nc.sync.dma_start(out=dtab_w[:].bitcast(I32), in_=dtab_words[0].bitcast(I32))
        nc.sync.dma_start(o2[:], offs2)
        nc.sync.dma_start(out=ground_t[:], in_=ground.rearrange("(p t) u -> p t u", t=PACK))
        load_scales(nc.sync, dtab_s, dtab_scales)
        nc.sync.dma_start(out=wor_raw[:], in_=wor.rearrange("(p j) c -> p j c", j=PACK))
        nc.sync.dma_start(out=res_t[:], in_=res.rearrange("(p t) u -> p t u", t=PACK))

        def deal(copy, dst, src, m0, s0, n):
            copy(dst[:, :, m0 : m0 + n, :].rearrange("p (h e) m j -> p h m j e", e=2),
                 src[:, :, PACK * s0 : PACK * (s0 + n)].rearrange("p j (m h e) -> p h m j e", h=2, e=2))

        def deal_rows(copy, dst, src, m0, s0, n):
            copy(dst[:, :, m0 : m0 + n, :],
                 src[:, :, PACK * s0 : PACK * (s0 + n)].rearrange("p j (m t) -> p t m j", t=PACK))

        w1b = tile("w1b", [P, PACK, P, PACK], BF16)
        g_s = tile("g_s", [P, J], U8)
        g_w = tile("g_w", [P, J], U16)
        dg_s = tile("dg_s", [P, J], U8)
        dg_w = tile("dg_w", [P, J], U16)
        nc.vector.tensor_copy(g_w[:], tab_w[:].indirect(o1[:]))
        nc.vector.tensor_copy(g_s[:], tab_s[:].indirect(o1[:]))
        deal_rows(nc.vector.tensor_copy, w1b, w1raw[0], 0, 0, 32)
        deal(nc.scalar.copy, w1b, w1raw[0], 32, 32, 32)
        deal_rows(nc.vector.tensor_copy, w1b, w1raw[1], 64, 0, 32)
        deal(nc.scalar.copy, w1b, w1raw[1], 96, 32, 32)
        w1c = tile("w1c", [P, R], U32)
        w1s = tile("w1s", [P, R], U8)

        def quant(codes, scales, src):
            nc.vector.quantize_mx(out=codes.bitcast(FP8X4), scales=scales, in_=src)

        w1flat = w1b[:].rearrange("p t m j -> p (t m j)")
        quant(w1c[:, 0:128], w1s[:, 0:128], w1flat[:, 0:512])
        quant(w1c[:, 128:256], w1s[:, 128:256], w1flat[:, 512:1024])
        quant(w1c[:, 256:512], w1s[:, 256:512], w1flat[:, 1024:2048])

        def first_mm(acc, words, scales, t):
            nc.tensor.matmul_mx(out=acc, lhsT=w1c[:, P * t : P * (t + 1)].bitcast(FP8X4), lhsT_scale=w1s[:, P * t : P * (t + 1)],
                                rhs=words[:].bitcast(FP4X4), rhs_scale=scales[:], start=True, stop=True)

        def times_gain(name, acc, t, tag=None):
            h = tile(name + "%d" % t, [P, J], F32, tag=tag)
            nc.scalar.activation(h[:], acc, ACT.Copy, scale=gain_t[:, t : t + 1])
            return h

        h1 = []
        for t in range(PACK):
            acc = bank("a%d" % t, t)
            first_mm(acc[:, 0:J], g_w, g_s, t)
            h1.append(times_gain("h1_", acc[:, 0:J], t))
        nc.vector.tensor_copy(dg_w[:], dtab_w[:].indirect(o1[:]))
        nc.vector.tensor_copy(dg_s[:], dtab_s[:].indirect(o1[:]))
        th1 = []
        ta = []
        for t in range(PACK):
            acc = bank("ta%d" % t, PACK + t)
            first_mm(acc[:, 0:J], dg_w, dg_s, t)
            ta.append(acc)
        nrs_t = tile("nrs_t", [P, PACK], F32)
        nc.gpsimd.tensor_scalar(nrs_t[:], rs_t[:], -1.0, 0.0, ALU.mult, ALU.add)

        worb = tile("worb", [P, PACK, P, PACK], BF16)
        slope = []
        for t in range(PACK):
            nc.vector.tensor_copy(page[t][:].indirect(o2[:]), h1[t][:])
            st = tile("s%d" % t, [P, U], F32)
            nc.gpsimd.tensor_tensor(st[:], page[t][:], ground_t[:, t, :], ALU.add)
            if t == 3:
                for g in range(4):
                    deal(nc.scalar.copy, worb, wor_raw, 32 * g, 32 * g, 32)
            ut = tile("u%d" % t, [P, U], F32)
            nc.scalar.activation(ut[:], st[:], ACT.Tanh)
            vt = tile("v%d" % t, [P, U], F32)
            nc.scalar.activation(vt[:], ut[:], ACT.Square)
            if t in (1, 2):
                th1.append(times_gain("th1_", ta[2 * t - 2][:, 0:J], 2 * t - 2, tag="u%d" % t))
            sl = tile("slope%d" % t, [P, U], F32)
            nc.scalar.activation(sl[:], vt[:], ACT.Identity, scale=nrs_t[:, t : t + 1], bias=rs_t[:, t : t + 1])
            slope.append(sl)
            if t in (1, 2):
                th1.append(times_gain("th1_", ta[2 * t - 1][:, 0:J], 2 * t - 1, tag="v%d" % t))

        worc = tile("worc", [P, F], U32)
        wors = tile("wors", [P, F], U8)

        fo = tile("fo", [P, PACK, U], BF16)
        for t in range(PACK):
            nc.vector.tensor_copy(tpage[t][:].indirect(o2[:]), th1[t][:])
            if t < PACK - 1:
                nc.gpsimd.tensor_tensor(fo[:, t, :], tpage[t][:], slope[t][:], ALU.mult)
            if t == 2:
                quant(worc[:], wors[:], worb[:].rearrange("p t m j -> p (t m j)"))
        last = PACK - 1
        nc.vector.tensor_tensor(fo[:, last, 0:CH], tpage[last][:, 0:CH], slope[last][:, 0:CH], ALU.mult)
        nc.vector.tensor_tensor(fo[:, last, CH:U], tpage[last][:, CH:U], slope[last][:, CH:U], ALU.mult)

        def weave(copy, dst, src):
            copy(dst.rearrange("p (c i) t -> p c t i", i=4), src.rearrange("p t (c i) -> p c t i", i=4))

        foc = [tile("foc%d" % c, [P, CH], U32) for c in range(NCH)]
        fos = [tile("fos%d" % c, [P, CH], U8) for c in range(NCH)]
        accs = []
        for c in range(NCH):
            cols = slice(CH * c, CH * (c + 1))
            fw = tile("fw%d" % c, [P, CH, PACK], BF16)
            weave(nc.vector.tensor_copy if c == 1 else nc.scalar.copy, fw[:], fo[:, :, cols])
            quant(foc[c][:], fos[c][:], fw[:].rearrange("p u t -> p (u t)"))
            acc = bank("yacc%d" % c, c)
            for t in range(PACK):
                nc.tensor.matmul_mx(out=acc[:, CH * t : CH * (t + 1)], lhsT=worc[:, P * t : P * (t + 1)].bitcast(FP8X4), lhsT_scale=wors[:, P * t : P * (t + 1)],
                                    rhs=foc[c][:].bitcast(FP8X4), rhs_scale=fos[c][:], start=True, stop=True)
            accs.append(acc)

        y = tile("y", [P, PACK, U], F32)
        yc = tile("yc", [P, U], U32)
        ys = tile("ys", [P, U], U8)
        outv = out_0.rearrange("(p t) u -> p t u", t=PACK)
        wordv = out_1[0].rearrange("p c r -> p (c r)").bitcast(I32)
        yws = []
        for c in range(NCH + 1):
            if c < NCH:
                cols = slice(CH * c, CH * (c + 1))
                nc.vector.tensor_tensor(y[:, :, cols], accs[c][:].rearrange("p (t u) -> p t u", t=PACK), res_t[:, :, cols], ALU.add)
                yw = tile("yw%d" % c, [P, CH, PACK], BF16)
                if c < NCH - 1:
                    weave(nc.scalar.copy, yw[:], y[:, :, cols])
                else:
                    weave(nc.scalar.copy, yw[:, 0 : CH // 2, :], y[:, :, U - CH : U - CH // 2])
                    weave(nc.vector.tensor_copy, yw[:, CH // 2 : CH, :], y[:, :, U - CH // 2 : U])
                yws.append(yw)
                if c % 2 == 1:
                    nc.sync.dma_start(out=outv[:, :, CH * (c - 1) : CH * (c + 1)], in_=y[:, :, CH * (c - 1) : CH * (c + 1)])
            if c > 0:
                pc = slice(CH * (c - 1), CH * c)
                quant(yc[:, pc], ys[:, pc], yws[c - 1][:].rearrange("p u t -> p (u t)"))
                if c == NCH - 1:
                    nc.sync.dma_start(out=wordv[:, 0 : CH * c], in_=yc[:, 0 : CH * c].bitcast(I32))
        nc.sync.dma_start(out=wordv[:, U - CH : U], in_=yc[:, U - CH : U].bitcast(I32))
        for q in range(4):
            eng = nc.scalar if q < 2 else nc.sync
            eng.dma_start(out=out_2[0, 4 * q : 4 * q + 4, :].bitcast(I32), in_=ys[32 * q : 32 * q + 4, :].bitcast(I32))
